import numpy as np
import ml_dtypes


def mxq(x, axis, fmt="e4m3"):
    dtype, down = {"e4m3": (ml_dtypes.float8_e4m3fn, 7), "e5m2": (ml_dtypes.float8_e5m2, 14)}[fmt]
    v = np.moveaxis(np.asarray(x, np.float32).astype(ml_dtypes.bfloat16).astype(np.float64), axis, -1)
    blocks = v.reshape(v.shape[:-1] + (-1, 32))
    amax = np.abs(blocks).max(-1, keepdims=True)
    byte = np.maximum(np.where(amax > 0, np.frexp(amax)[1] - 1 + 127, 0) - down, 1)
    scale = np.exp2(byte - 127.0)
    codes = (blocks / scale).astype(np.float32).astype(dtype).astype(np.float64)
    return np.moveaxis((codes * scale).reshape(v.shape), -1, axis)


WIDE = False


def mx_kscale(k):
    if not WIDE:
        return np.ones(k)
    levels = np.array([10, -10, 5, -5, 0])
    if k % 512:
        return np.exp2(np.random.permutation(np.resize(levels, k // 32))).repeat(32)
    a = np.empty((k // 512, 16))
    for p in range(k // 512):
        a[p, :8] = np.random.permutation(np.resize(levels, 8))
        for g in range(8):
            far = levels[np.abs(levels - a[p, g]) >= 10]
            a[p, g + 8] = far[np.random.randint(len(far))]
    return np.exp2(a.ravel()).repeat(32)


def f64(x):
    return np.asarray(x).astype(np.float64)


def striped(idx):
    return np.tile(np.asarray(idx).reshape(-1, 16).T, (8, 1)).astype(np.uint16)


def unstriped(offs):
    return offs[:16].T.reshape(-1).astype(np.int64)


E2M1 = np.array([0.0, 0.5, 1.0, 1.5, 2.0, 3.0, 4.0, 6.0, -0.0, -0.5, -1.0, -1.5, -2.0, -3.0, -4.0, -6.0])


def pack_weight(w, fmt):
    k, n = w.shape
    w = f64(np.asarray(w, np.float32).astype(ml_dtypes.bfloat16)).reshape(k // 32, 32, n)
    amax = np.abs(w).max(1)
    if fmt == "e4m3":
        byte = np.frexp(amax)[1] - 1 + 127 - 7
    else:
        mant, ex = np.frexp(amax / 6.0)
        byte = np.where(mant > 0.5, ex, ex - 1) + 127
    byte = np.clip(np.where(amax > 0, byte, 1), 1, 254)
    scaled = (w * np.exp2(127.0 - byte)[:, None, :]).reshape(k, n).astype(np.float32)
    by_word = np.ascontiguousarray(scaled.reshape(k // 512, 128, 4, n).transpose(0, 1, 3, 2))
    if fmt == "e4m3":
        words = by_word.astype(ml_dtypes.float8_e4m3fn).view(np.uint8)
    else:
        c = by_word.astype(ml_dtypes.float4_e2m1fn).view(np.uint8) & 0xF
        words = (c[..., 0::2] | (c[..., 1::2] << 4)).reshape(k // 512, 128, 2 * n)
    return np.ascontiguousarray(words), np.ascontiguousarray(byte.astype(np.uint8).reshape(k // 512, 16, n))


def unpack_weight(words, scales, fmt):
    g, _, n = scales.shape
    words = np.ascontiguousarray(words).reshape(g, 128, n, -1)
    if fmt == "e4m3":
        vals = words.view(ml_dtypes.float8_e4m3fn).astype(np.float64)
    else:
        nib = np.empty((g, 128, n, 4), np.uint8)
        nib[..., 0::2] = words & 0xF
        nib[..., 1::2] = words >> 4
        vals = E2M1[nib]
    vals = vals * np.repeat(np.exp2(scales.astype(np.float64) - 127.0), 8, axis=1)[..., None]
    return vals.transpose(0, 1, 3, 2).reshape(g * 512, n)


D, E, U, T, I, G, Q = 512, 512, 512, 2048, 512, 64, 128


def setup_inputs():
    n = np.random.standard_normal
    idx = np.random.permutation(T)[:I]
    idx2 = np.random.permutation(U)[:G]
    fd = mx_kscale(D)
    fe = mx_kscale(E)
    keysp = pack_weight(n((D, T)) / fd[:, None], "e2m1")
    valsp = pack_weight(n((E, T)) / fe[:, None], "e2m1")
    return {
        "pquery": (n((D, Q)) * 0.8 / np.sqrt(D) * fd[:, None]).astype(np.float32),
        "pgsum": (n((D, U)) / fd[:, None]).astype(np.float32),
        "query": (n((D, Q)) * 0.7 / np.sqrt(D) * fd[:, None]).astype(np.float32),
        "keys_words": keysp[0],
        "keys_scales": keysp[1],
        "gout": (n((E, Q)) * 1 / np.sqrt(E) * fe[:, None]).astype(np.float32),
        "vals_words": valsp[0],
        "vals_scales": valsp[1],
        "old": (0.5 * n((Q, T))).astype(np.float32),
        "offs": striped(idx),
        "offs2": striped(idx2),
    }


def reference(pquery, pgsum, query, keys_words, keys_scales, gout, vals_words, vals_scales, old, offs, offs2):
    idx = unstriped(offs)
    idx2 = unstriped(offs2)
    keysu = unpack_weight(keys_words, keys_scales, "e2m1")
    valsu = unpack_weight(vals_words, vals_scales, "e2m1")
    pqueryq = mxq(f64(pquery), 0, "e4m3")
    pgsumq = mxq(f64(pgsum), 0, "e4m3")
    b = pqueryq.T @ pgsumq
    m1 = np.max(b, axis=1, keepdims=True)
    pb = np.exp(b - m1)
    z = np.sum(pb, axis=1, keepdims=True)
    queryq = mxq(f64(query), 0, "e4m3")
    keysidxg = keysu[:, idx]
    a = queryq.T @ keysidxg
    pa = np.exp(a)
    s = pa.reshape(Q, G, I // G).sum(axis=2)
    mo = np.exp(b[:, idx2] - m1)
    sh = mo / s
    sr = np.repeat(sh, I // G, axis=1)
    goutq = mxq(f64(gout), 0, "e4m3")
    valsidxg = valsu[:, idx]
    c1 = goutq.T @ valsidxg
    dsr = 1.0 / z * c1 * pa
    dsh = dsr.reshape(Q, G, I // G).sum(axis=2)
    ds = dsh * mo / np.square(s) * (-1.0)
    r1 = np.repeat(ds, I // G, axis=1)
    dpa = 1.0 / z * c1 * sr + r1
    da = dpa * pa
    gs = da * 2048.0
    gf = np.zeros((Q, T))
    gf[:, idx] = gs
    y = f64(old) + gf
    return y

from contextlib import ExitStack

import concourse.mybir as mybir

D, E, U, T, I, G, Q = 512, 512, 512, 2048, 512, 64, 128
FLOPS = 2 * Q * (D * U + D * I + E * I)

F32 = mybir.dt.float32
BF16 = mybir.dt.bfloat16
I32 = mybir.dt.int32
U32 = mybir.dt.uint32
U16 = mybir.dt.uint16
U8 = mybir.dt.uint8
FP8X4 = mybir.dt.float8_e4m3fn_x4
FP4X4 = mybir.dt.float4_e2m1fn_x4
ALU = mybir.AluOpType
ACT = mybir.ActivationFunctionType
AX = mybir.AxisListType

P = 128
PACK = 4
PAGE = I // G
OUT_CUTS = (0, 256, 512, 1024, 1536, 2048)


def load_rows(nc, pool, rows, name, tag):
    width = rows.shape[1]
    raw = pool.tile([P, PACK, width], F32, name=name, tag=tag, align_bytes=64)
    nc.sync.dma_start(out=raw[:], in_=rows.rearrange("(p j) w -> p j w", j=PACK))
    return raw


def load_scales(queues, plane, scales):
    by_row = scales[0].rearrange("(q r) t -> r q t", r=4)
    for r in range(4):
        queues[r].dma_start(out=plane[r:P:32, :].bitcast(I32), in_=by_row[r].bitcast(I32))


def weave(nc, engine, pool, raw, name):
    width = raw.shape[2]
    woven = pool.tile([P, width, PACK], BF16, name=name, align_bytes=64)
    dst = woven[:].rearrange("p (c i) t -> p c t i", i=4)
    src = raw[:].rearrange("p t (c i) -> p c t i", i=4)
    if engine == "s":
        nc.scalar.copy(out=dst, in_=src)
    elif engine == "v":
        nc.vector.tensor_copy(out=dst, in_=src)
    else:
        nc.gpsimd.tensor_scalar(out=dst, in0=src, scalar1=1.0, scalar2=0.0, op0=ALU.mult, op1=ALU.add)
    return woven


def quantize(nc, woven, codes, plane):
    nc.vector.quantize_mx(out=codes.bitcast(FP8X4), scales=plane, in_=woven[:].rearrange("p w j -> p (w j)"))


def tile_attend_bopened_a_kernel(tc, pquery, pgsum, query, keys_words, keys_scales, gout, vals_words, vals_scales, old, offs, offs2, out):
    nc = tc.nc
    with ExitStack() as ctx:
        lists = ctx.enter_context(tc.tile_pool(name="lists", bufs=1))
        sb = ctx.enter_context(tc.tile_pool(name="sb", bufs=1))
        psum = ctx.enter_context(tc.psum_pool(name="psum", bufs=1))
        offs_t = lists.tile([P, I // 16], U16, name="offs_t")
        offs2_t = lists.tile([P, G // 16], U16, name="offs2_t")
        ks_t = sb.tile([P, T], U8, name="ks_t", tag="ks_t", align_bytes=64)
        vs_t = sb.tile([P, T], U8, name="vs_t", tag="vs_t", align_bytes=64)
        kw_t = sb.tile([P, T], U16, name="kw_t", tag="kw_t", align_bytes=64)
        vw_t = sb.tile([P, T], U16, name="vw_t", tag="vw_t", align_bytes=64)
        gf = sb.tile([P, T], F32, name="gf", align_bytes=64)
        res = sb.tile([P, T], F32, name="res", align_bytes=64)
        warm = sb.tile([P, 1], F32, name="warm", align_bytes=64)
        ksg = sb.tile([P, I], U8, name="ksg", align_bytes=64)
        kwg = sb.tile([P, I], U16, name="kwg", align_bytes=64)
        vsg = sb.tile([P, I], U8, name="vsg", align_bytes=64)
        vwg = sb.tile([P, I], U16, name="vwg", align_bytes=64)
        q_c = sb.tile([P, Q], U32, name="q_c", align_bytes=64)
        q_s = sb.tile([P, Q], U8, name="q_s", align_bytes=64)
        pq_c = sb.tile([P, Q], U32, name="pq_c", align_bytes=64)
        pq_s = sb.tile([P, Q], U8, name="pq_s", align_bytes=64)
        go_c = sb.tile([P, Q], U32, name="go_c", align_bytes=64)
        go_s = sb.tile([P, Q], U8, name="go_s", align_bytes=64)
        pg_c = sb.tile([P, U], U32, name="pg_c", align_bytes=64)
        pg_s = sb.tile([P, U], U8, name="pg_s", align_bytes=64)
        pa = sb.tile([P, I], F32, name="pa", align_bytes=64)
        s = sb.tile([P, G], F32, name="s", align_bytes=64)
        rs = sb.tile([P, G], F32, name="rs", align_bytes=64)
        b = sb.tile([P, U], F32, name="b", align_bytes=64)
        m1 = sb.tile([P, 1], F32, name="m1", align_bytes=64)
        neg_m1 = sb.tile([P, 1], F32, name="neg_m1", align_bytes=64)
        bg = sb.tile([P, G], F32, name="bg", align_bytes=64)
        pb = sb.tile([P, U], F32, name="pb", align_bytes=64)
        z = sb.tile([P, 1], F32, name="z", align_bytes=64)
        mo = sb.tile([P, G], F32, name="mo", align_bytes=64)
        cp = sb.tile([P, I], F32, name="cp", align_bytes=64)
        sh = sb.tile([P, G], F32, name="sh", align_bytes=64)
        shz = sb.tile([P, G], F32, name="shz", align_bytes=64)
        u = sb.tile([P, G], F32, name="u", align_bytes=64)
        rz = sb.tile([P, 1], F32, name="rz", align_bytes=64)
        share = sb.tile([P, I], F32, name="share", align_bytes=64)
        mean = sb.tile([P, G], F32, name="mean", align_bytes=64)
        dev = sb.tile([P, I], F32, name="dev", align_bytes=64)
        wz = sb.tile([P, 1], F32, name="wz", tag="pg1_raw", align_bytes=64)
        a_ps = psum.tile([P, 512], F32, name="a_ps")
        b_ps = psum.tile([P, 512], F32, name="b_ps")
        c_ps = psum.tile([P, 512], F32, name="c_ps")
        nc.vector.memset(ks_t[:].bitcast(I32), 0)
        nc.vector.memset(wz[:], 0.0)
        nc.vector.memset(vs_t[:].bitcast(I32), 0)
        nc.vector.memset(gf[:], 0.0)
        nc.sync.dma_start(offs_t[:], offs)
        nc.sync.dma_start(offs2_t[:], offs2)
        load_scales([nc.scalar] * 4, ks_t, keys_scales)
        nc.sync.dma_start(out=kw_t[:].bitcast(I32), in_=keys_words[0].bitcast(I32))
        q_raw = load_rows(nc, sb, query, "q_raw", "q_raw")
        pg0_raw = load_rows(nc, sb, pgsum[:, 0:256], "pg0_raw", "pg0_raw")
        nc.sync.dma_start(out=vw_t[:].bitcast(I32), in_=vals_words[0].bitcast(I32))
        load_scales([nc.gpsimd, nc.gpsimd, nc.gpsimd, nc.sync], vs_t, vals_scales)
        nc.scalar.activation(out=warm[:], in_=wz[:], func=ACT.Exp)
        pg1_raw = load_rows(nc, sb, pgsum[:, 256:512], "pg1_raw", "pg1_raw")
        nc.vector.tensor_copy(kwg[:], kw_t[:].indirect(offs_t[:]))
        q_w = weave(nc, "s", sb, q_raw, "q_w")
        pq_raw = load_rows(nc, sb, pquery, "pq_raw", "q_raw")
        nc.vector.tensor_copy(ksg[:], ks_t[:].indirect(offs_t[:]))
        go_raw = load_rows(nc, sb, gout, "go_raw", "ks_t")
        quantize(nc, q_w, q_c[:], q_s[:])
        nc.tensor.matmul_mx(out=a_ps[:], lhsT=q_c[:].bitcast(FP8X4), lhsT_scale=q_s[:], rhs=kwg[:].bitcast(FP4X4), rhs_scale=ksg[:], start=True, stop=True)
        pg0_w = weave(nc, "s", sb, pg0_raw, "pg0_w")
        nc.vector.tensor_copy(vwg[:], vw_t[:].indirect(offs_t[:]))
        nc.scalar.activation(out=pa[:], in_=a_ps[:], func=ACT.Exp)
        nc.vector.tensor_copy(vsg[:], vs_t[:].indirect(offs_t[:]))
        old_h = []
        for h, tag in enumerate(("vw_t", "pg0_raw")):
            half = sb.tile([P, 1024], F32, name="old%d" % h, tag=tag, align_bytes=64)
            nc.sync.dma_start(out=half[:], in_=old[:, 1024 * h:1024 * h + 1024])
            old_h.append(half)
        pg1_w = weave(nc, "s", sb, pg1_raw, "pg1_w")
        quantize(nc, pg0_w, pg_c[:, 0:256], pg_s[:, 0:256])
        quantize(nc, pg1_w, pg_c[:, 256:512], pg_s[:, 256:512])
        nc.vector.tensor_reduce(out=s[:], in_=pa[:].rearrange("p (g j) -> p g j", j=PAGE), axis=AX.X, op=ALU.add)
        pq_w = weave(nc, "s", sb, pq_raw, "pq_w")
        quantize(nc, pq_w, pq_c[:], pq_s[:])
        nc.tensor.matmul_mx(out=b_ps[:], lhsT=pq_c[:].bitcast(FP8X4), lhsT_scale=pq_s[:], rhs=pg_c[:].bitcast(FP8X4), rhs_scale=pg_s[:], start=True, stop=True)
        nc.vector.reciprocal(out=rs[:], in_=s[:])
        go_w = weave(nc, "s", sb, go_raw, "go_w")
        nc.vector.tensor_scalar(out=b[:], in0=b_ps[:], scalar1=1.0, scalar2=None, op0=ALU.mult, op1=ALU.max, accum_out=m1[:])
        quantize(nc, go_w, go_c[:], go_s[:])
        nc.tensor.matmul_mx(out=c_ps[:], lhsT=go_c[:].bitcast(FP8X4), lhsT_scale=go_s[:], rhs=vwg[:].bitcast(FP4X4), rhs_scale=vsg[:], start=True, stop=True)
        nc.scalar.activation(out=neg_m1[:], in_=m1[:], func=ACT.Copy, scale=-1.0)
        nc.vector.tensor_copy(bg[:], b[:].indirect(offs2_t[:]))
        nc.scalar.activation(out=mo[:], in_=bg[:], func=ACT.Exp, bias=neg_m1[:])
        nc.scalar.activation(out=pb[:], in_=b[:], func=ACT.Exp, bias=neg_m1[:], accum_out=z[:])
        nc.vector.tensor_tensor(out=cp[:, 0:512], in0=c_ps[:, 0:512], in1=pa[:, 0:512], op=ALU.mult)
        nc.vector.scalar_tensor_tensor(out=sh[:], in0=mo[:], scalar=2048.0, in1=rs[:], op0=ALU.mult, op1=ALU.mult)
        nc.vector.tensor_reduce(out=u[:, 0:64], in_=cp[:, 0:512].rearrange("p (g j) -> p g j", j=PAGE), axis=AX.X, op=ALU.add)
        nc.vector.reciprocal(out=rz[:], in_=z[:])
        nc.vector.tensor_tensor(out=share[:, 0:512].rearrange("p (g j) -> p g j", j=PAGE), in0=pa[:, 0:512].rearrange("p (g j) -> p g j", j=PAGE), in1=sh[:, 0:64].unsqueeze(2).to_broadcast([P, 64, PAGE]), op=ALU.mult)
        nc.vector.scalar_tensor_tensor(out=mean[:, 0:64], in0=u[:, 0:64], scalar=rz[:], in1=rs[:, 0:64], op0=ALU.mult, op1=ALU.mult)
        nc.vector.scalar_tensor_tensor(out=dev[:, 0:512].rearrange("p (g j) -> p g j", j=PAGE), in0=c_ps[:, 0:512].rearrange("p (g j) -> p g j", j=PAGE), scalar=rz[:], in1=mean[:, 0:64].unsqueeze(2).to_broadcast([P, 64, PAGE]), op0=ALU.mult, op1=ALU.subtract)
        nc.vector.tensor_tensor(gf[:].indirect(offs_t[:]), dev[:], share[:], ALU.mult)
        for lo, hi in zip(OUT_CUTS[:-1], OUT_CUTS[1:]):
            nc.vector.tensor_tensor(out=res[:, lo:hi], in0=gf[:, lo:hi], in1=old_h[lo // 1024][:, lo % 1024:lo % 1024 + hi - lo], op=ALU.add)
            nc.sync.dma_start(out=out[:, lo:hi], in_=res[:, lo:hi])
